import numpy as np
import ml_dtypes


def mxq(x, axis, fmt="e4m3"):
    dtype, down = {"e4m3": (ml_dtypes.float8_e4m3fn, 7), "e5m2": (ml_dtypes.float8_e5m2, 14)}[fmt]
    v = np.moveaxis(np.asarray(x, np.float32).astype(ml_dtypes.bfloat16).astype(np.float64), axis, -1)
    blocks = v.reshape(v.shape[:-1] + (-1, 32))
    amax = np.abs(blocks).max(-1, keepdims=True)
    byte = np.maximum(np.where(amax > 0, np.frexp(amax)[1] - 1 + 127, 0) - down, 1)
    scale = np.exp2(byte - 127.0)
    codes = (blocks / scale).astype(np.float32).astype(dtype).astype(np.float64)
    return np.moveaxis((codes * scale).reshape(v.shape), -1, axis)


WIDE = False


def mx_kscale(k):
    if not WIDE:
        return np.ones(k)
    levels = np.array([10, -10, 5, -5, 0])
    if k % 512:
        return np.exp2(np.random.permutation(np.resize(levels, k // 32))).repeat(32)
    a = np.empty((k // 512, 16))
    for p in range(k // 512):
        a[p, :8] = np.random.permutation(np.resize(levels, 8))
        for g in range(8):
            far = levels[np.abs(levels - a[p, g]) >= 10]
            a[p, g + 8] = far[np.random.randint(len(far))]
    return np.exp2(a.ravel()).repeat(32)


def f64(x):
    return np.asarray(x).astype(np.float64)


def striped(idx):
    return np.tile(idx.reshape(-1, 16).T, (8, 1)).astype(np.uint16)


def unstriped(offs):
    return offs[:16].T.reshape(-1).astype(np.int64)


E2M1 = np.array([0.0, 0.5, 1.0, 1.5, 2.0, 3.0, 4.0, 6.0, -0.0, -0.5, -1.0, -1.5, -2.0, -3.0, -4.0, -6.0])


def pack_weight(w, fmt):
    k, n = w.shape
    w = f64(np.asarray(w, np.float32).astype(ml_dtypes.bfloat16)).reshape(k // 32, 32, n)
    amax = np.abs(w).max(1)
    if fmt == "e4m3":
        byte = np.frexp(amax)[1] - 1 + 127 - 7
    else:
        mant, ex = np.frexp(amax / 6.0)
        byte = np.where(mant > 0.5, ex, ex - 1) + 127
    byte = np.clip(np.where(amax > 0, byte, 1), 1, 254)
    scaled = (w * np.exp2(127.0 - byte)[:, None, :]).reshape(k, n).astype(np.float32)
    by_word = np.ascontiguousarray(scaled.reshape(k // 512, 128, 4, n).transpose(0, 1, 3, 2))
    if fmt == "e4m3":
        words = by_word.astype(ml_dtypes.float8_e4m3fn).view(np.uint8)
    else:
        c = by_word.astype(ml_dtypes.float4_e2m1fn).view(np.uint8) & 0xF
        words = (c[..., 0::2] | (c[..., 1::2] << 4)).reshape(k // 512, 128, 2 * n)
    return np.ascontiguousarray(words), np.ascontiguousarray(byte.astype(np.uint8).reshape(k // 512, 16, n))


def unpack_weight(words, scales, fmt):
    g, _, n = scales.shape
    words = np.ascontiguousarray(words).reshape(g, 128, n, -1)
    if fmt == "e4m3":
        vals = words.view(ml_dtypes.float8_e4m3fn).astype(np.float64)
    else:
        nib = np.empty((g, 128, n, 4), np.uint8)
        nib[..., 0::2] = words & 0xF
        nib[..., 1::2] = words >> 4
        vals = E2M1[nib]
    vals = vals * np.repeat(np.exp2(scales.astype(np.float64) - 127.0), 8, axis=1)[..., None]
    return vals.transpose(0, 1, 3, 2).reshape(g * 512, n)


def gelu(v):
    return 0.5 * v * (1.0 + np.tanh(np.sqrt(2.0 / np.pi) * (v + 0.044715 * v**3)))


def bf(x):
    return np.asarray(x, np.float32).astype(ml_dtypes.bfloat16)


def planes(Y):
    n, m = Y.shape
    b = f64(bf(Y)).reshape(n // 32, 32, m)
    amax = np.abs(b).max(1)
    byte = np.clip(np.where(amax > 0, np.frexp(amax)[1] - 1 + 127 - 7, 1), 1, 254)
    codes = (b * np.exp2(127.0 - byte)[:, None, :]).reshape(n, m).astype(np.float32).astype(ml_dtypes.float8_e4m3fn).view(np.uint8)
    words = codes.reshape(n // 512, 128, 4, m).transpose(0, 1, 3, 2)
    return np.ascontiguousarray(words), np.ascontiguousarray(byte.astype(np.uint8).reshape(n // 512, 16, m))


K, H, N, T, S, P = 1536, 1024, 512, 4096, 1024, 512

def setup_inputs():
    n = np.random.standard_normal
    s = mx_kscale(K)[:, None]
    u = mx_kscale(H)[:, None]
    d = {}
    d["tab_words"], d["tab_scales"] = pack_weight(n((K, T)) * s, "e4m3")
    d["offs"] = striped(np.random.permutation(T)[:S])
    d["w1"] = (1.2 * n((K, H)) / K**0.5 / s).astype(np.float32)
    d["shift"] = (0.6 * n(H)).astype(np.float32)
    d["gain"] = (np.exp(0.3 * n(H)) * u[:, 0]).astype(np.float32)
    w4 = n((H, N)) / H**0.5 / u * np.exp(0.8 * n(N))[None, :]
    d["w4_words"], d["w4_scales"] = pack_weight(w4, "e2m1")
    d["pos1"] = striped(np.random.permutation(S)[:P])
    d["pos2"] = striped(np.random.permutation(S)[:P])
    return d

def reference(tab_words, tab_scales, offs, w1, shift, gain, w4_words, w4_scales, pos1, pos2):
    v = unpack_weight(tab_words, tab_scales, "e4m3")[:, unstriped(offs)]
    a = (mxq(f64(w1), 0, "e4m3").T @ v) + f64(shift)[:, None]
    h = 0.5 * a * (1 + np.tanh((2 / np.pi)**0.5 * (a + 0.044715 * a**3)))
    h = h * f64(gain)[:, None]
    hq = mxq(h, 0, "e4m3")
    g2 = np.square(unpack_weight(w4_words, w4_scales, "e2m1").T @ hq)
    y = np.sqrt(1 + (g2[:, unstriped(pos1)] + g2[:, unstriped(pos2)]))
    words, scales = planes(y)
    return y, words, scales

@@ -1,0 +1,248 @@
+from contextlib import ExitStack
+
+import concourse.mybir as mybir
+
+K, H, N, T, S, M = 1536, 1024, 512, 4096, 1024, 512
+FLOPS = 2 * K * H * S + 2 * H * N * S
+
+F32 = mybir.dt.float32
+BF16 = mybir.dt.bfloat16
+I32 = mybir.dt.int32
+U32 = mybir.dt.uint32
+U16 = mybir.dt.uint16
+U8 = mybir.dt.uint8
+FP8X4 = mybir.dt.float8_e4m3fn_x4
+FP4X4 = mybir.dt.float4_e2m1fn_x4
+ACT = mybir.ActivationFunctionType
+ALU = mybir.AluOpType
+
+P = 128
+PACK = 4
+PASS = P * PACK
+KP = K // PASS
+HP = H // PASS
+BANK = 512
+HALVES = S // BANK
+QUADS = 4
+CAST_PLAN = [[[("vector", 0, 4)], [("vector", 0, 4)], [("vector", 0, 2), ("scalar", 2, 4)]], [[("vector", 0, 4)], [("scalar", 0, 4)], [("vector", 0, 2), ("scalar", 2, 4)]]]
+H_PIECES = [[[256, 256], [512]], [[256, 256], [512]]]
+H_STEP = 256
+M_PIECES = [256, 256]
+
+
+def tile_list_tread_edge_loudness_kernel(
+    tc, tab_words, tab_scales, offs, w1, shift, gain, w4_words, w4_scales, pos1, pos2, out_0, out_1, out_2
+):
+    nc = tc.nc
+    with ExitStack() as ctx:
+        keep = ctx.enter_context(tc.tile_pool(name="keep", bufs=1))
+        ring = ctx.enter_context(tc.tile_pool(name="ring", bufs=2))
+        psum = ctx.enter_context(tc.psum_pool(name="psum", bufs=1))
+
+        idx = keep.tile([P, S // 16], U16, name="idx")
+        nc.sync.dma_start(idx[:], offs)
+
+        lead = keep.tile([P, M // 16], U16, name="lead")
+        nc.sync.dma_start(lead[:], pos1)
+        trail = keep.tile([P, M // 16], U16, name="trail")
+        nc.sync.dma_start(trail[:], pos2)
+        w4_raw = []
+        for b in range(HP):
+            raw = keep.tile([P, 2 * N], U8, name="w4_raw%d" % b)
+            nc.sync.dma_start(raw[:].bitcast(I32), w4_words[b].bitcast(I32))
+            w4_raw.append(raw)
+        shift_t = keep.tile([P, HP, PACK], F32, name="shift_t")
+        nc.sync.dma_start(shift_t[:], shift.rearrange("(b p t) -> p b t", p=P, t=PACK))
+        gain_t = keep.tile([P, HP, PACK], F32, name="gain_t")
+        nc.sync.dma_start(gain_t[:], gain.rearrange("(b p t) -> p b t", p=P, t=PACK))
+
+        scale_rows = keep.tile([P, T], U8, name="scale_rows", align_bytes=64)
+        nc.gpsimd.memset(scale_rows[:].bitcast(I32), 0)
+        w4_sraw = keep.tile([P, HP, N], U8, name="w4_sraw")
+        nc.gpsimd.memset(w4_sraw[:].bitcast(I32), 0)
+
+        table = []
+        for a in range(KP):
+            words = keep.tile([P, T], I32, name="table%d" % a, align_bytes=64)
+            nc.sync.dma_start(words[:], tab_words[a].rearrange("p n i -> p (n i)").bitcast(I32))
+            table.append(words)
+            if a == 0:
+                for q in range(QUADS):
+                    nc.gpsimd.dma_start(
+                        scale_rows[32 * q : 32 * q + 4 * KP, :].bitcast(I32),
+                        tab_scales[:, 4 * q : 4 * q + 4, :].bitcast(I32),
+                    )
+
+        w1_raw = {}
+        for b in range(HP):
+            for a in range(KP):
+                raw = keep.tile([P, PACK, PASS], F32, name="w1_raw%d%d" % (b, a))
+                src = w1[a * PASS : (a + 1) * PASS, b * PASS : (b + 1) * PASS]
+                nc.sync.dma_start(raw[:], src.rearrange("(p j) c -> p j c", j=PACK))
+                w1_raw[b, a] = raw
+                if (b, a) == (0, 0):
+                    for q in range(QUADS):
+                        nc.gpsimd.dma_start(
+                            w4_sraw[32 * q : 32 * q + 4, :, :].bitcast(I32),
+                            w4_scales[:, 4 * q : 4 * q + 4, :].rearrange("b r n -> r b n").bitcast(I32),
+                        )
+
+        warm = keep.tile([P, 1], F32, name="warm")
+        nc.gpsimd.memset(warm[:], 0.0)
+        warmed = keep.tile([P, 1], F32, name="warmed")
+        nc.scalar.activation(warmed[:], warm[:], ACT.Gelu_apprx_tanh)
+
+        w4_code = keep.tile([P, HP, PACK, P, 2], U8, name="w4_code", align_bytes=64)
+        for b in range(HP):
+            nc.vector.tensor_copy(
+                w4_code[:, b].rearrange("p t q e -> p q t e"),
+                w4_raw[b][:].rearrange("p (q t e) -> p q t e", t=PACK, e=2),
+            )
+        v_code = []
+        for a in range(KP):
+            picked = keep.tile([P, S], U32, name="v_code%d" % a, align_bytes=64)
+            nc.vector.tensor_copy(picked[:], table[a][:].bitcast(U32).indirect(idx[:]))
+            v_code.append(picked)
+            if a == 0:
+                v_scale = keep.tile([P, S], U8, name="v_scale", align_bytes=64)
+                nc.vector.tensor_copy(v_scale[:], scale_rows[:].indirect(idx[:]))
+        w4_scale = keep.tile([P, HP, PACK, P], U8, name="w4_scale", align_bytes=64)
+        nc.vector.tensor_copy(
+            w4_scale[:].rearrange("p b t q -> p b q t"),
+            w4_sraw[:].rearrange("p b (q t) -> p b q t", t=PACK),
+        )
+
+        def quantise_w1(b, a):
+            code = keep.tile([P, PACK, P], U32, name="w1_code%d%d" % (b, a), align_bytes=64)
+            scale = keep.tile([P, PACK, P], U8, name="w1_scale%d%d" % (b, a), align_bytes=64)
+            for engine, t0, t1 in CAST_PLAN[b][a]:
+                grouped = ring.tile([P, t1 - t0, P, PACK], BF16, name="w1_grouped", bufs=3, align_bytes=64)
+                dst = grouped[:].rearrange("p t q j -> p q j t")
+                src = w1_raw[b, a][:].rearrange("p j (q t) -> p q j t", t=PACK)[:, :, :, t0:t1]
+                if engine == "vector":
+                    nc.vector.tensor_copy(dst, src)
+                else:
+                    nc.scalar.copy(dst, src)
+                nc.vector.quantize_mx(
+                    out=code[:, t0:t1, :].rearrange("p t q -> p (t q)").bitcast(FP8X4),
+                    scales=scale[:, t0:t1, :].rearrange("p t q -> p (t q)"),
+                    in_=grouped[:].rearrange("p t q j -> p (t q j)"),
+                )
+            return code, scale
+
+
+        def first_product(b):
+            weights = [quantise_w1(b, a) for a in range(KP)]
+            banks = {}
+            for half in range(HALVES):
+                cols = slice(half * BANK, (half + 1) * BANK)
+                for a, (code, scale) in enumerate(weights):
+                    for t in range(PACK):
+                        if a == 0:
+                            banks[half, t] = psum.tile([P, BANK], F32, name="bank%d%d" % (half, t))
+                        nc.tensor.matmul_mx(
+                            out=banks[half, t][:],
+                            lhsT=code[:, t, :].bitcast(FP8X4),
+                            lhsT_scale=scale[:, t, :],
+                            rhs=v_code[a][:, cols].bitcast(FP8X4),
+                            rhs_scale=v_scale[4 * a : P, cols],
+                            start=(a == 0),
+                            stop=(a == KP - 1),
+                        )
+            return banks
+
+        def activate(b, banks):
+            acts = []
+            for half in range(HALVES):
+                c0 = 0
+                for width in H_PIECES[b][half]:
+                    act = ring.tile([P, PACK, width], F32, name="act", bufs=4)
+                    for t in range(PACK):
+                        nc.scalar.activation(
+                            act[:, t, :],
+                            banks[half, t][:, c0 : c0 + width],
+                            ACT.Gelu_apprx_tanh,
+                            bias=shift_t[:, b, t : t + 1],
+                        )
+                    acts.append((half, c0, width, act))
+                    c0 = c0 + width
+            return acts
+
+        h_code, h_scale = {}, {}
+
+        def quantise_h(b, acts):
+            for half in range(HALVES):
+                h_code[b, half] = keep.tile([P, BANK], U32, name="h_code%d%d" % (b, half), align_bytes=64)
+                h_scale[b, half] = keep.tile([P, BANK], U8, name="h_scale%d%d" % (b, half), align_bytes=64)
+            factor = gain_t[:, b, :].rearrange("p (c t i) -> p c t i", c=1, i=1)
+            for half, c0, width, act in acts:
+                step = min(width, H_STEP)
+                for s0 in range(0, width, step):
+                    cols = slice(c0 + s0, c0 + s0 + step)
+                    h_bf = ring.tile([P, step, PACK], BF16, name="h_bf", bufs=3, align_bytes=64)
+                    nc.vector.tensor_tensor(
+                        h_bf[:].rearrange("p (c i) t -> p c t i", i=4),
+                        act[:, :, s0 : s0 + step].rearrange("p t (c i) -> p c t i", i=4),
+                        factor.to_broadcast([P, step // 4, PACK, 4]),
+                        ALU.mult,
+                    )
+                    nc.vector.quantize_mx(
+                        out=h_code[b, half][:, cols].bitcast(FP8X4),
+                        scales=h_scale[b, half][:, cols],
+                        in_=h_bf[:].rearrange("p n t -> p (n t)"),
+                    )
+
+        acts0 = activate(0, first_product(0))
+        banks1 = first_product(1)
+        quantise_h(0, acts0)
+        quantise_h(1, activate(1, banks1))
+
+        g2 = [keep.tile([P, S], F32, name="g2_%d" % t) for t in range(PACK)]
+        for half in range(HALVES):
+            for t in range(PACK):
+                bank = psum.tile([P, BANK], F32, name="bank%d%d" % (half, t))
+                for b in range(HP):
+                    nc.tensor.matmul_mx(
+                        out=bank[:],
+                        lhsT=w4_code[:, b, t].rearrange("p q e -> p (q e)").bitcast(FP4X4),
+                        lhsT_scale=w4_scale[:, b, t, :],
+                        rhs=h_code[b, half][:].bitcast(FP8X4),
+                        rhs_scale=h_scale[b, half][:],
+                        start=(b == 0),
+                        stop=(b == HP - 1),
+                    )
+                nc.scalar.activation(g2[t][:, half * BANK : (half + 1) * BANK], bank[:], ACT.Square)
+
+        y_code = keep.tile([P, M], U32, name="y_code", align_bytes=64)
+        y_scale = keep.tile([P, M], U8, name="y_scale", align_bytes=64)
+        y_rows = out_0.rearrange("(p t) m -> p t m", t=PACK)
+        code_rows = out_1[0].rearrange("p m t -> p (m t)").bitcast(I32)
+        m0 = 0
+        for piece, width in enumerate(M_PIECES):
+            cols = slice(m0, m0 + width)
+            lists = slice(m0 // 16, (m0 + width) // 16)
+            m0 = m0 + width
+            y = keep.tile([P, PACK, width], F32, name="y%d" % piece)
+            for t in range(PACK):
+                first = ring.tile([P, width], F32, name="first", bufs=3)
+                nc.vector.tensor_copy(first[:], g2[t][:].indirect(lead[:, lists]))
+                both = ring.tile([P, width], F32, name="both", bufs=3)
+                nc.vector.tensor_tensor(both[:], g2[t][:].indirect(trail[:, lists]), first[:], ALU.add)
+                nc.scalar.activation(y[:, t, :], both[:], ACT.Sqrt, bias=1.0)
+            nc.sync.dma_start(y_rows[:, :, cols], y[:])
+            y_bf = ring.tile([P, width, PACK], BF16, name="y_bf", bufs=2, align_bytes=64)
+            dst = y_bf[:].rearrange("p (c i) t -> p c t i", i=4)
+            src = y[:].rearrange("p t (c i) -> p c t i", i=4)
+            if piece == len(M_PIECES) - 1:
+                nc.vector.tensor_copy(dst, src)
+            else:
+                nc.scalar.copy(dst, src)
+            nc.vector.quantize_mx(
+                out=y_code[:, cols].bitcast(FP8X4),
+                scales=y_scale[:, cols],
+                in_=y_bf[:].rearrange("p m t -> p (m t)"),
+            )
+            nc.sync.dma_start(code_rows[:, cols], y_code[:, cols].bitcast(I32))
+        for q in range(QUADS):
+            queue = nc.scalar if q % 2 else nc.sync
+            queue.dma_start(out_2[0, 4 * q : 4 * q + 4, :].bitcast(I32), y_scale[32 * q : 32 * q + 4, :].bitcast(I32))

@@ -24,9 +24,9 @@ HP = H // PASS
 BANK = 512
 HALVES = S // BANK
 QUADS = 4
-CAST_PLAN = [[[("vector", 0, 4)], [("vector", 0, 4)], [("vector", 0, 2), ("scalar", 2, 4)]], [[("vector", 0, 4)], [("scalar", 0, 4)], [("vector", 0, 2), ("scalar", 2, 4)]]]
-H_PIECES = [[[256, 256], [512]], [[256, 256], [512]]]
-H_STEP = 256
+CAST_PLAN = [[[[("vector", 0, 4)]], [[("vector", 0, 4)]], [[("vector", 0, 2)], [("scalar", 2, 4)]]], [[[("vector", 0, 4)]], [[("vector", 0, 2), ("scalar", 2, 4)]], [[("vector", 0, 2), ("scalar", 2, 4)]]]]
+H_PIECES = [[[512], [512]], [[512], [512]]]
+H_STEP = [[512, 512], [512, 512]]
 M_PIECES = [256, 256]
 
 
@@ -57,7 +57,7 @@ def tile_list_tread_edge_loudness_kernel(
         nc.sync.dma_start(gain_t[:], gain.rearrange("(b p t) -> p b t", p=P, t=PACK))
 
         scale_rows = keep.tile([P, T], U8, name="scale_rows", align_bytes=64)
-        nc.gpsimd.memset(scale_rows[:].bitcast(I32), 0)
+        nc.vector.memset(scale_rows[:].bitcast(I32), 0)
         w4_sraw = keep.tile([P, HP, N], U8, name="w4_sraw")
         nc.gpsimd.memset(w4_sraw[:].bitcast(I32), 0)
 
@@ -68,7 +68,7 @@ def tile_list_tread_edge_loudness_kernel(
             table.append(words)
             if a == 0:
                 for q in range(QUADS):
-                    nc.gpsimd.dma_start(
+                    nc.sync.dma_start(
                         scale_rows[32 * q : 32 * q + 4 * KP, :].bitcast(I32),
                         tab_scales[:, 4 * q : 4 * q + 4, :].bitcast(I32),
                     )
@@ -82,7 +82,7 @@ def tile_list_tread_edge_loudness_kernel(
                 w1_raw[b, a] = raw
                 if (b, a) == (0, 0):
                     for q in range(QUADS):
-                        nc.gpsimd.dma_start(
+                        nc.sync.dma_start(
                             w4_sraw[32 * q : 32 * q + 4, :, :].bitcast(I32),
                             w4_scales[:, 4 * q : 4 * q + 4, :].rearrange("b r n -> r b n").bitcast(I32),
                         )
@@ -115,24 +115,28 @@ def tile_list_tread_edge_loudness_kernel(
         def quantise_w1(b, a):
             code = keep.tile([P, PACK, P], U32, name="w1_code%d%d" % (b, a), align_bytes=64)
             scale = keep.tile([P, PACK, P], U8, name="w1_scale%d%d" % (b, a), align_bytes=64)
-            for engine, t0, t1 in CAST_PLAN[b][a]:
-                grouped = ring.tile([P, t1 - t0, P, PACK], BF16, name="w1_grouped", bufs=3, align_bytes=64)
-                dst = grouped[:].rearrange("p t q j -> p q j t")
-                src = w1_raw[b, a][:].rearrange("p j (q t) -> p q j t", t=PACK)[:, :, :, t0:t1]
-                if engine == "vector":
-                    nc.vector.tensor_copy(dst, src)
+            for group in CAST_PLAN[b][a]:
+                g0, g1 = group[0][1], group[-1][2]
+                if (b, a) == (HP - 1, KP - 1):
+                    grouped = keep.tile([P, g1 - g0, P, PACK], BF16, name="w1_last", tag="handover", align_bytes=64)
                 else:
-                    nc.scalar.copy(dst, src)
+                    grouped = ring.tile([P, g1 - g0, P, PACK], BF16, name="w1_grouped", bufs=3, align_bytes=64)
+                for engine, t0, t1 in group:
+                    dst = grouped[:, t0 - g0 : t1 - g0].rearrange("p t q j -> p q j t")
+                    src = w1_raw[b, a][:].rearrange("p j (q t) -> p q j t", t=PACK)[:, :, :, t0:t1]
+                    if engine == "vector":
+                        nc.vector.tensor_copy(dst, src)
+                    else:
+                        nc.scalar.copy(dst, src)
                 nc.vector.quantize_mx(
-                    out=code[:, t0:t1, :].rearrange("p t q -> p (t q)").bitcast(FP8X4),
-                    scales=scale[:, t0:t1, :].rearrange("p t q -> p (t q)"),
+                    out=code[:, g0:g1, :].rearrange("p t q -> p (t q)").bitcast(FP8X4),
+                    scales=scale[:, g0:g1, :].rearrange("p t q -> p (t q)"),
                     in_=grouped[:].rearrange("p t q j -> p (t q j)"),
                 )
             return code, scale
 
 
-        def first_product(b):
-            weights = [quantise_w1(b, a) for a in range(KP)]
+        def first_product(weights):
             banks = {}
             for half in range(HALVES):
                 cols = slice(half * BANK, (half + 1) * BANK)
@@ -156,7 +160,7 @@ def tile_list_tread_edge_loudness_kernel(
             for half in range(HALVES):
                 c0 = 0
                 for width in H_PIECES[b][half]:
-                    act = ring.tile([P, PACK, width], F32, name="act", bufs=4)
+                    act = ring.tile([P, PACK, width], F32, name="act", bufs=3)
                     for t in range(PACK):
                         nc.scalar.activation(
                             act[:, t, :],
@@ -176,10 +180,13 @@ def tile_list_tread_edge_loudness_kernel(
                 h_scale[b, half] = keep.tile([P, BANK], U8, name="h_scale%d%d" % (b, half), align_bytes=64)
             factor = gain_t[:, b, :].rearrange("p (c t i) -> p c t i", c=1, i=1)
             for half, c0, width, act in acts:
-                step = min(width, H_STEP)
+                step = min(width, H_STEP[b][half])
                 for s0 in range(0, width, step):
                     cols = slice(c0 + s0, c0 + s0 + step)
-                    h_bf = ring.tile([P, step, PACK], BF16, name="h_bf", bufs=3, align_bytes=64)
+                    if (b, half) == (0, 1):
+                        h_bf = keep.tile([P, step, PACK], BF16, name="h_after", tag="handover", align_bytes=64)
+                    else:
+                        h_bf = ring.tile([P, step, PACK], BF16, name="h_bf", bufs=2, align_bytes=64)
                     nc.vector.tensor_tensor(
                         h_bf[:].rearrange("p (c i) t -> p c t i", i=4),
                         act[:, :, s0 : s0 + step].rearrange("p t (c i) -> p c t i", i=4),
@@ -192,8 +199,10 @@ def tile_list_tread_edge_loudness_kernel(
                         in_=h_bf[:].rearrange("p n t -> p (n t)"),
                     )
 
-        acts0 = activate(0, first_product(0))
-        banks1 = first_product(1)
+        banks0 = first_product([quantise_w1(0, a) for a in range(KP)])
+        weights1 = [quantise_w1(1, a) for a in range(KP)]
+        acts0 = activate(0, banks0)
+        banks1 = first_product(weights1)
         quantise_h(0, acts0)
         quantise_h(1, activate(1, banks1))
 
@@ -224,9 +233,9 @@ def tile_list_tread_edge_loudness_kernel(
             m0 = m0 + width
             y = keep.tile([P, PACK, width], F32, name="y%d" % piece)
             for t in range(PACK):
-                first = ring.tile([P, width], F32, name="first", bufs=3)
+                first = ring.tile([P, width], F32, name="first", bufs=2)
                 nc.vector.tensor_copy(first[:], g2[t][:].indirect(lead[:, lists]))
-                both = ring.tile([P, width], F32, name="both", bufs=3)
+                both = ring.tile([P, width], F32, name="both", bufs=2)
                 nc.vector.tensor_tensor(both[:], g2[t][:].indirect(trail[:, lists]), first[:], ALU.add)
                 nc.scalar.activation(y[:, t, :], both[:], ACT.Sqrt, bias=1.0)
             nc.sync.dma_start(y_rows[:, :, cols], y[:])

@@ -24,9 +24,9 @@ HP = H // PASS
 BANK = 512
 HALVES = S // BANK
 QUADS = 4
-CAST_PLAN = [[[[("vector", 0, 4)]], [[("vector", 0, 4)]], [[("vector", 0, 2)], [("scalar", 2, 4)]]], [[[("vector", 0, 4)]], [[("vector", 0, 2), ("scalar", 2, 4)]], [[("vector", 0, 2), ("scalar", 2, 4)]]]]
-H_PIECES = [[[512], [512]], [[512], [512]]]
-H_STEP = [[512, 512], [512, 512]]
+CAST_PLAN = [[[[("scalar", 0, 2), ("scalar", 2, 4)]], [[("scalar", 0, 2), ("scalar", 2, 4)]], [[("vector", 0, 2)], [("scalar", 2, 4)]]], [[[("vector", 0, 2), ("vector", 2, 4)]], [[("vector", 0, 2)], [("scalar", 2, 4)]], [[("vector", 0, 2)], [("scalar", 2, 4)]]]]
+H_PIECES = [[[512], [512]], [[512], [256, 256]]]
+H_STEP = [[512, 512], [512, 256]]
 M_PIECES = [256, 256]
 
 
@@ -42,50 +42,67 @@ def tile_list_tread_edge_loudness_kernel(
         idx = keep.tile([P, S // 16], U16, name="idx")
         nc.sync.dma_start(idx[:], offs)
 
-        lead = keep.tile([P, M // 16], U16, name="lead")
-        nc.sync.dma_start(lead[:], pos1)
-        trail = keep.tile([P, M // 16], U16, name="trail")
-        nc.sync.dma_start(trail[:], pos2)
-        w4_raw = []
-        for b in range(HP):
-            raw = keep.tile([P, 2 * N], U8, name="w4_raw%d" % b)
-            nc.sync.dma_start(raw[:].bitcast(I32), w4_words[b].bitcast(I32))
-            w4_raw.append(raw)
+        scale_rows = keep.tile([P, T], U8, name="scale_rows", align_bytes=64)
+        rows = tab_scales.rearrange("a q n -> (a q) n").bitcast(I32)
+        nc.sync.dma_start(scale_rows[16:32, :].bitcast(I32), rows[0:16, :])
+        nc.sync.dma_start(scale_rows[32:64, :].bitcast(I32), rows[16:48, :])
+        nc.vector.memset(scale_rows[0:16, :].bitcast(I32), 0)
+        nc.vector.memset(scale_rows[64:P, :].bitcast(I32), 0)
+        picked_rows = keep.tile([P, S], U8, name="picked_rows", align_bytes=64)
+        nc.vector.tensor_copy(picked_rows[:], scale_rows[:].indirect(idx[:]))
+
+        table, w1_raw, v_scale = {}, {}, {}
+
+        def load_table(a):
+            table[a] = keep.tile([P, T], I32, name="table%d" % a, align_bytes=64)
+            nc.sync.dma_start(table[a][:], tab_words[a].rearrange("p n i -> p (n i)").bitcast(I32))
+
+        def load_w1(b, a):
+            w1_raw[b, a] = keep.tile([P, PACK, PASS], F32, name="w1_raw%d%d" % (b, a))
+            src = w1[a * PASS : (a + 1) * PASS, b * PASS : (b + 1) * PASS]
+            nc.sync.dma_start(w1_raw[b, a][:], src.rearrange("(p j) c -> p j c", j=PACK))
+
+        def place_scales(moves):
+            for a, q in moves:
+                first_row = 16 + 16 * a + 4 * q
+                nc.sync.dma_start(
+                    v_scale[a][32 * q : 32 * q + 4, :].bitcast(I32),
+                    picked_rows[first_row : first_row + 4, :].bitcast(I32),
+                )
+
+        w4_sraw = keep.tile([P, HP, N], U8, name="w4_sraw")
+        nc.gpsimd.memset(w4_sraw[:].bitcast(I32), 0)
+        for a in range(KP):
+            v_scale[a] = keep.tile([P, S], U8, name="v_scale%d" % a, align_bytes=64)
+            nc.gpsimd.memset(v_scale[a][:].bitcast(I32), 0)
+        moves = [(a, q) for a in range(KP) for q in range(QUADS)]
+
+        load_table(0)
+        w4_raw = keep.tile([P, HP, 2 * N], U8, name="w4_raw")
+        nc.sync.dma_start(w4_raw[:].bitcast(I32), w4_words.rearrange("b p n -> p b n").bitcast(I32))
         shift_t = keep.tile([P, HP, PACK], F32, name="shift_t")
         nc.sync.dma_start(shift_t[:], shift.rearrange("(b p t) -> p b t", p=P, t=PACK))
         gain_t = keep.tile([P, HP, PACK], F32, name="gain_t")
         nc.sync.dma_start(gain_t[:], gain.rearrange("(b p t) -> p b t", p=P, t=PACK))
-
-        scale_rows = keep.tile([P, T], U8, name="scale_rows", align_bytes=64)
-        nc.vector.memset(scale_rows[:].bitcast(I32), 0)
-        w4_sraw = keep.tile([P, HP, N], U8, name="w4_sraw")
-        nc.gpsimd.memset(w4_sraw[:].bitcast(I32), 0)
-
-        table = []
-        for a in range(KP):
-            words = keep.tile([P, T], I32, name="table%d" % a, align_bytes=64)
-            nc.sync.dma_start(words[:], tab_words[a].rearrange("p n i -> p (n i)").bitcast(I32))
-            table.append(words)
-            if a == 0:
-                for q in range(QUADS):
-                    nc.sync.dma_start(
-                        scale_rows[32 * q : 32 * q + 4 * KP, :].bitcast(I32),
-                        tab_scales[:, 4 * q : 4 * q + 4, :].bitcast(I32),
-                    )
-
-        w1_raw = {}
-        for b in range(HP):
-            for a in range(KP):
-                raw = keep.tile([P, PACK, PASS], F32, name="w1_raw%d%d" % (b, a))
-                src = w1[a * PASS : (a + 1) * PASS, b * PASS : (b + 1) * PASS]
-                nc.sync.dma_start(raw[:], src.rearrange("(p j) c -> p j c", j=PACK))
-                w1_raw[b, a] = raw
-                if (b, a) == (0, 0):
-                    for q in range(QUADS):
-                        nc.sync.dma_start(
-                            w4_sraw[32 * q : 32 * q + 4, :, :].bitcast(I32),
-                            w4_scales[:, 4 * q : 4 * q + 4, :].rearrange("b r n -> r b n").bitcast(I32),
-                        )
+        load_w1(0, 0)
+        for q in range(QUADS):
+            nc.sync.dma_start(
+                w4_sraw[32 * q : 32 * q + 4, :, :].bitcast(I32),
+                w4_scales[:, 4 * q : 4 * q + 4, :].rearrange("b r n -> r b n").bitcast(I32),
+            )
+        load_table(1)
+        load_w1(0, 1)
+        place_scales(moves[:6])
+        load_table(2)
+        place_scales(moves[6:])
+        load_w1(0, 2)
+        load_w1(1, 0)
+        load_w1(1, 1)
+        load_w1(1, 2)
+        lead = keep.tile([P, M // 16], U16, name="lead")
+        nc.sync.dma_start(lead[:], pos1)
+        trail = keep.tile([P, M // 16], U16, name="trail")
+        nc.sync.dma_start(trail[:], pos2)
 
         warm = keep.tile([P, 1], F32, name="warm")
         nc.gpsimd.memset(warm[:], 0.0)
@@ -95,21 +112,18 @@ def tile_list_tread_edge_loudness_kernel(
         w4_code = keep.tile([P, HP, PACK, P, 2], U8, name="w4_code", align_bytes=64)
         for b in range(HP):
             nc.vector.tensor_copy(
-                w4_code[:, b].rearrange("p t q e -> p q t e"),
-                w4_raw[b][:].rearrange("p (q t e) -> p q t e", t=PACK, e=2),
+                w4_code[:, b],
+                w4_raw[:, b, :].rearrange("p (q t e) -> p t q e", t=PACK, e=2),
             )
         v_code = []
         for a in range(KP):
             picked = keep.tile([P, S], U32, name="v_code%d" % a, align_bytes=64)
             nc.vector.tensor_copy(picked[:], table[a][:].bitcast(U32).indirect(idx[:]))
             v_code.append(picked)
-            if a == 0:
-                v_scale = keep.tile([P, S], U8, name="v_scale", align_bytes=64)
-                nc.vector.tensor_copy(v_scale[:], scale_rows[:].indirect(idx[:]))
         w4_scale = keep.tile([P, HP, PACK, P], U8, name="w4_scale", align_bytes=64)
         nc.vector.tensor_copy(
-            w4_scale[:].rearrange("p b t q -> p b q t"),
-            w4_sraw[:].rearrange("p b (q t) -> p b q t", t=PACK),
+            w4_scale[:],
+            w4_sraw[:].rearrange("p b (q t) -> p b t q", t=PACK),
         )
 
         def quantise_w1(b, a):
@@ -117,7 +131,7 @@ def tile_list_tread_edge_loudness_kernel(
             scale = keep.tile([P, PACK, P], U8, name="w1_scale%d%d" % (b, a), align_bytes=64)
             for group in CAST_PLAN[b][a]:
                 g0, g1 = group[0][1], group[-1][2]
-                if (b, a) == (HP - 1, KP - 1):
+                if (b, a, g1) == (HP - 1, KP - 1, PACK):
                     grouped = keep.tile([P, g1 - g0, P, PACK], BF16, name="w1_last", tag="handover", align_bytes=64)
                 else:
                     grouped = ring.tile([P, g1 - g0, P, PACK], BF16, name="w1_grouped", bufs=3, align_bytes=64)
@@ -149,7 +163,7 @@ def tile_list_tread_edge_loudness_kernel(
                             lhsT=code[:, t, :].bitcast(FP8X4),
                             lhsT_scale=scale[:, t, :],
                             rhs=v_code[a][:, cols].bitcast(FP8X4),
-                            rhs_scale=v_scale[4 * a : P, cols],
+                            rhs_scale=v_scale[a][:, cols],
                             start=(a == 0),
                             stop=(a == KP - 1),
                         )
@@ -188,9 +202,9 @@ def tile_list_tread_edge_loudness_kernel(
                     else:
                         h_bf = ring.tile([P, step, PACK], BF16, name="h_bf", bufs=2, align_bytes=64)
                     nc.vector.tensor_tensor(
-                        h_bf[:].rearrange("p (c i) t -> p c t i", i=4),
-                        act[:, :, s0 : s0 + step].rearrange("p t (c i) -> p c t i", i=4),
-                        factor.to_broadcast([P, step // 4, PACK, 4]),
+                        h_bf[:].rearrange("p (c i) t -> p c t i", i=2),
+                        act[:, :, s0 : s0 + step].rearrange("p t (c i) -> p c t i", i=2),
+                        factor.to_broadcast([P, step // 2, PACK, 2]),
                         ALU.mult,
                     )
                     nc.vector.quantize_mx(
@@ -235,13 +249,13 @@ def tile_list_tread_edge_loudness_kernel(
             for t in range(PACK):
                 first = ring.tile([P, width], F32, name="first", bufs=2)
                 nc.vector.tensor_copy(first[:], g2[t][:].indirect(lead[:, lists]))
-                both = ring.tile([P, width], F32, name="both", bufs=2)
+                both = ring.tile([P, width], F32, name="both", bufs=4)
                 nc.vector.tensor_tensor(both[:], g2[t][:].indirect(trail[:, lists]), first[:], ALU.add)
                 nc.scalar.activation(y[:, t, :], both[:], ACT.Sqrt, bias=1.0)
             nc.sync.dma_start(y_rows[:, :, cols], y[:])
             y_bf = ring.tile([P, width, PACK], BF16, name="y_bf", bufs=2, align_bytes=64)
-            dst = y_bf[:].rearrange("p (c i) t -> p c t i", i=4)
-            src = y[:].rearrange("p t (c i) -> p c t i", i=4)
+            dst = y_bf[:].rearrange("p (c i) t -> p c t i", i=2)
+            src = y[:].rearrange("p t (c i) -> p c t i", i=2)
             if piece == len(M_PIECES) - 1:
                 nc.vector.tensor_copy(dst, src)
             else:

@@ -24,9 +24,9 @@ HP = H // PASS
 BANK = 512
 HALVES = S // BANK
 QUADS = 4
-CAST_PLAN = [[[[("scalar", 0, 2), ("scalar", 2, 4)]], [[("scalar", 0, 2), ("scalar", 2, 4)]], [[("vector", 0, 2)], [("scalar", 2, 4)]]], [[[("vector", 0, 2), ("vector", 2, 4)]], [[("vector", 0, 2)], [("scalar", 2, 4)]], [[("vector", 0, 2)], [("scalar", 2, 4)]]]]
+CAST_PLAN = [[("scalar", "scalar"), ("scalar", "scalar"), ("vector", "scalar")], [("vector", "vector"), ("vector", "scalar"), ("vector", "scalar")]]
 H_PIECES = [[[512], [512]], [[512], [256, 256]]]
-H_STEP = [[512, 512], [512, 256]]
+H_STEP = 256
 M_PIECES = [256, 256]
 
 
@@ -126,29 +126,33 @@ def tile_list_tread_edge_loudness_kernel(
             w4_sraw[:].rearrange("p b (q t) -> p b t q", t=PACK),
         )
 
-        def quantise_w1(b, a):
+        def round_w1(b, a):
+            pairs = []
+            for pair, engine in enumerate(CAST_PLAN[b][a]):
+                if (b, a, pair) == (HP - 1, KP - 1, 1):
+                    grouped = keep.tile([P, 2, P, PACK], BF16, name="w1_last", tag="handover", align_bytes=64)
+                else:
+                    grouped = ring.tile([P, 2, P, PACK], BF16, name="w1_grouped", bufs=4, align_bytes=64)
+                dst = grouped[:].rearrange("p t q j -> p q j t")
+                src = w1_raw[b, a][:].rearrange("p j (q t) -> p q j t", t=PACK)[:, :, :, 2 * pair : 2 * pair + 2]
+                if engine == "vector":
+                    nc.vector.tensor_copy(dst, src)
+                else:
+                    nc.scalar.copy(dst, src)
+                pairs.append(grouped)
+            return pairs
+
+        def quantise_w1(b, a, pairs):
             code = keep.tile([P, PACK, P], U32, name="w1_code%d%d" % (b, a), align_bytes=64)
             scale = keep.tile([P, PACK, P], U8, name="w1_scale%d%d" % (b, a), align_bytes=64)
-            for group in CAST_PLAN[b][a]:
-                g0, g1 = group[0][1], group[-1][2]
-                if (b, a, g1) == (HP - 1, KP - 1, PACK):
-                    grouped = keep.tile([P, g1 - g0, P, PACK], BF16, name="w1_last", tag="handover", align_bytes=64)
-                else:
-                    grouped = ring.tile([P, g1 - g0, P, PACK], BF16, name="w1_grouped", bufs=3, align_bytes=64)
-                for engine, t0, t1 in group:
-                    dst = grouped[:, t0 - g0 : t1 - g0].rearrange("p t q j -> p q j t")
-                    src = w1_raw[b, a][:].rearrange("p j (q t) -> p q j t", t=PACK)[:, :, :, t0:t1]
-                    if engine == "vector":
-                        nc.vector.tensor_copy(dst, src)
-                    else:
-                        nc.scalar.copy(dst, src)
+            for pair, grouped in enumerate(pairs):
+                slots = slice(2 * pair, 2 * pair + 2)
                 nc.vector.quantize_mx(
-                    out=code[:, g0:g1, :].rearrange("p t q -> p (t q)").bitcast(FP8X4),
-                    scales=scale[:, g0:g1, :].rearrange("p t q -> p (t q)"),
+                    out=code[:, slots, :].rearrange("p t q -> p (t q)").bitcast(FP8X4),
+                    scales=scale[:, slots, :].rearrange("p t q -> p (t q)"),
                     in_=grouped[:].rearrange("p t q j -> p (t q j)"),
                 )
             return code, scale
-
 
         def first_product(weights):
             banks = {}
@@ -189,32 +193,35 @@ def tile_list_tread_edge_loudness_kernel(
         h_code, h_scale = {}, {}
 
         def quantise_h(b, acts):
+            factor = gain_t[:, b, :].rearrange("p (c t i) -> p c t i", c=1, i=1)
             for half in range(HALVES):
                 h_code[b, half] = keep.tile([P, BANK], U32, name="h_code%d%d" % (b, half), align_bytes=64)
                 h_scale[b, half] = keep.tile([P, BANK], U8, name="h_scale%d%d" % (b, half), align_bytes=64)
-            factor = gain_t[:, b, :].rearrange("p (c t i) -> p c t i", c=1, i=1)
-            for half, c0, width, act in acts:
-                step = min(width, H_STEP[b][half])
-                for s0 in range(0, width, step):
-                    cols = slice(c0 + s0, c0 + s0 + step)
-                    if (b, half) == (0, 1):
-                        h_bf = keep.tile([P, step, PACK], BF16, name="h_after", tag="handover", align_bytes=64)
-                    else:
-                        h_bf = ring.tile([P, step, PACK], BF16, name="h_bf", bufs=2, align_bytes=64)
-                    nc.vector.tensor_tensor(
-                        h_bf[:].rearrange("p (c i) t -> p c t i", i=2),
-                        act[:, :, s0 : s0 + step].rearrange("p t (c i) -> p c t i", i=2),
-                        factor.to_broadcast([P, step // 2, PACK, 2]),
-                        ALU.mult,
-                    )
+                if (b, half) == (0, 1):
+                    h_bf = keep.tile([P, BANK, PACK], BF16, name="h_after", tag="handover", align_bytes=64)
+                else:
+                    h_bf = ring.tile([P, BANK, PACK], BF16, name="h_bf", bufs=2, align_bytes=64)
+                for act_half, c0, width, act in acts:
+                    if act_half == half:
+                        for s0 in range(0, width, H_STEP):
+                            nc.vector.tensor_tensor(
+                                h_bf[:, c0 + s0 : c0 + s0 + H_STEP, :].rearrange("p (c i) t -> p c t i", i=2),
+                                act[:, :, s0 : s0 + H_STEP].rearrange("p t (c i) -> p c t i", i=2),
+                                factor.to_broadcast([P, H_STEP // 2, PACK, 2]),
+                                ALU.mult,
+                            )
+                for s0 in range(0, BANK, H_STEP):
+                    cols = slice(s0, s0 + H_STEP)
                     nc.vector.quantize_mx(
                         out=h_code[b, half][:, cols].bitcast(FP8X4),
                         scales=h_scale[b, half][:, cols],
-                        in_=h_bf[:].rearrange("p n t -> p (n t)"),
+                        in_=h_bf[:, cols, :].rearrange("p n t -> p (n t)"),
                     )
 
-        banks0 = first_product([quantise_w1(0, a) for a in range(KP)])
-        weights1 = [quantise_w1(1, a) for a in range(KP)]
+        banks0 = first_product([quantise_w1(0, a, round_w1(0, a)) for a in range(KP)])
+        weights1 = [quantise_w1(1, 0, round_w1(1, 0))]
+        rounded = [round_w1(1, a) for a in range(1, KP)]
+        weights1.extend(quantise_w1(1, a, rounded[a - 1]) for a in range(1, KP))
         acts0 = activate(0, banks0)
         banks1 = first_product(weights1)
         quantise_h(0, acts0)
@@ -241,16 +248,18 @@ def tile_list_tread_edge_loudness_kernel(
         y_rows = out_0.rearrange("(p t) m -> p t m", t=PACK)
         code_rows = out_1[0].rearrange("p m t -> p (m t)").bitcast(I32)
         m0 = 0
+        first = {}
         for piece, width in enumerate(M_PIECES):
             cols = slice(m0, m0 + width)
             lists = slice(m0 // 16, (m0 + width) // 16)
             m0 = m0 + width
             y = keep.tile([P, PACK, width], F32, name="y%d" % piece)
             for t in range(PACK):
-                first = ring.tile([P, width], F32, name="first", bufs=2)
-                nc.vector.tensor_copy(first[:], g2[t][:].indirect(lead[:, lists]))
-                both = ring.tile([P, width], F32, name="both", bufs=4)
-                nc.vector.tensor_tensor(both[:], g2[t][:].indirect(trail[:, lists]), first[:], ALU.add)
+                if piece == 0:
+                    first[t] = keep.tile([P, M], F32, name="first%d" % t)
+                    nc.vector.tensor_copy(first[t][:], g2[t][:].indirect(lead[:]))
+                both = keep.tile([P, width], F32, name="both%d" % ((t + 2 * piece) % PACK))
+                nc.vector.tensor_tensor(both[:], g2[t][:].indirect(trail[:, lists]), first[t][:, cols], ALU.add)
                 nc.scalar.activation(y[:, t, :], both[:], ACT.Sqrt, bias=1.0)
             nc.sync.dma_start(y_rows[:, :, cols], y[:])
             y_bf = ring.tile([P, width, PACK], BF16, name="y_bf", bufs=2, align_bytes=64)

from contextlib import ExitStack

import concourse.mybir as mybir

K, H, N, T, S, M = 1536, 1024, 512, 4096, 1024, 512
FLOPS = 2 * K * H * S + 2 * H * N * S

F32 = mybir.dt.float32
BF16 = mybir.dt.bfloat16
I32 = mybir.dt.int32
U32 = mybir.dt.uint32
U16 = mybir.dt.uint16
U8 = mybir.dt.uint8
FP8X4 = mybir.dt.float8_e4m3fn_x4
FP4X4 = mybir.dt.float4_e2m1fn_x4
ACT = mybir.ActivationFunctionType
ALU = mybir.AluOpType

P = 128
PACK = 4
PASS = P * PACK
KP = K // PASS
HP = H // PASS
BANK = 512
HALVES = S // BANK
QUADS = 4
CAST_PLAN = [[("scalar", "scalar"), ("scalar", "scalar"), ("vector", "scalar")], [("vector", "vector"), ("vector", "scalar"), ("vector", "scalar")]]
H_PIECES = [[[512], [512]], [[512], [256, 256]]]
H_STEP = 256
M_PIECES = [256, 256]


def tile_list_tread_edge_loudness_kernel(
    tc, tab_words, tab_scales, offs, w1, shift, gain, w4_words, w4_scales, pos1, pos2, out_0, out_1, out_2
):
    nc = tc.nc
    with ExitStack() as ctx:
        keep = ctx.enter_context(tc.tile_pool(name="keep", bufs=1))
        ring = ctx.enter_context(tc.tile_pool(name="ring", bufs=2))
        psum = ctx.enter_context(tc.psum_pool(name="psum", bufs=1))

        idx = keep.tile([P, S // 16], U16, name="idx")
        nc.sync.dma_start(idx[:], offs)

        scale_rows = keep.tile([P, T], U8, name="scale_rows", align_bytes=64)
        rows = tab_scales.rearrange("a q n -> (a q) n").bitcast(I32)
        nc.sync.dma_start(scale_rows[16:32, :].bitcast(I32), rows[0:16, :])
        nc.sync.dma_start(scale_rows[32:64, :].bitcast(I32), rows[16:48, :])
        nc.vector.memset(scale_rows[0:16, :].bitcast(I32), 0)
        nc.vector.memset(scale_rows[64:P, :].bitcast(I32), 0)
        picked_rows = keep.tile([P, S], U8, name="picked_rows", align_bytes=64)
        nc.vector.tensor_copy(picked_rows[:], scale_rows[:].indirect(idx[:]))

        table, w1_raw, v_scale = {}, {}, {}

        def load_table(a):
            table[a] = keep.tile([P, T], I32, name="table%d" % a, align_bytes=64)
            nc.sync.dma_start(table[a][:], tab_words[a].rearrange("p n i -> p (n i)").bitcast(I32))

        def load_w1(b, a):
            w1_raw[b, a] = keep.tile([P, PACK, PASS], F32, name="w1_raw%d%d" % (b, a))
            src = w1[a * PASS : (a + 1) * PASS, b * PASS : (b + 1) * PASS]
            nc.sync.dma_start(w1_raw[b, a][:], src.rearrange("(p j) c -> p j c", j=PACK))

        def place_scales(moves):
            for a, q in moves:
                first_row = 16 + 16 * a + 4 * q
                nc.sync.dma_start(
                    v_scale[a][32 * q : 32 * q + 4, :].bitcast(I32),
                    picked_rows[first_row : first_row + 4, :].bitcast(I32),
                )

        w4_sraw = keep.tile([P, HP, N], U8, name="w4_sraw")
        nc.gpsimd.memset(w4_sraw[:].bitcast(I32), 0)
        for a in range(KP):
            v_scale[a] = keep.tile([P, S], U8, name="v_scale%d" % a, align_bytes=64)
            nc.gpsimd.memset(v_scale[a][:].bitcast(I32), 0)
        moves = [(a, q) for a in range(KP) for q in range(QUADS)]

        load_table(0)
        w4_raw = keep.tile([P, HP, 2 * N], U8, name="w4_raw")
        nc.sync.dma_start(w4_raw[:].bitcast(I32), w4_words.rearrange("b p n -> p b n").bitcast(I32))
        shift_t = keep.tile([P, HP, PACK], F32, name="shift_t")
        nc.sync.dma_start(shift_t[:], shift.rearrange("(b p t) -> p b t", p=P, t=PACK))
        gain_t = keep.tile([P, HP, PACK], F32, name="gain_t")
        nc.sync.dma_start(gain_t[:], gain.rearrange("(b p t) -> p b t", p=P, t=PACK))
        load_w1(0, 0)
        for q in range(QUADS):
            nc.sync.dma_start(
                w4_sraw[32 * q : 32 * q + 4, :, :].bitcast(I32),
                w4_scales[:, 4 * q : 4 * q + 4, :].rearrange("b r n -> r b n").bitcast(I32),
            )
        load_table(1)
        load_w1(0, 1)
        place_scales(moves[:6])
        load_table(2)
        place_scales(moves[6:])
        load_w1(0, 2)
        load_w1(1, 0)
        load_w1(1, 1)
        load_w1(1, 2)
        lead = keep.tile([P, M // 16], U16, name="lead")
        nc.sync.dma_start(lead[:], pos1)
        trail = keep.tile([P, M // 16], U16, name="trail")
        nc.sync.dma_start(trail[:], pos2)

        warm = keep.tile([P, 1], F32, name="warm")
        nc.gpsimd.memset(warm[:], 0.0)
        warmed = keep.tile([P, 1], F32, name="warmed")
        nc.scalar.activation(warmed[:], warm[:], ACT.Gelu_apprx_tanh)

        w4_code = keep.tile([P, HP, PACK, P, 2], U8, name="w4_code", align_bytes=64)
        for b in range(HP):
            nc.vector.tensor_copy(
                w4_code[:, b],
                w4_raw[:, b, :].rearrange("p (q t e) -> p t q e", t=PACK, e=2),
            )
        v_code = []
        for a in range(KP):
            picked = keep.tile([P, S], U32, name="v_code%d" % a, align_bytes=64)
            nc.vector.tensor_copy(picked[:], table[a][:].bitcast(U32).indirect(idx[:]))
            v_code.append(picked)
        w4_scale = keep.tile([P, HP, PACK, P], U8, name="w4_scale", align_bytes=64)
        nc.vector.tensor_copy(
            w4_scale[:],
            w4_sraw[:].rearrange("p b (q t) -> p b t q", t=PACK),
        )

        def round_w1(b, a):
            pairs = []
            for pair, engine in enumerate(CAST_PLAN[b][a]):
                if (b, a, pair) == (HP - 1, KP - 1, 1):
                    grouped = keep.tile([P, 2, P, PACK], BF16, name="w1_last", tag="handover", align_bytes=64)
                else:
                    grouped = ring.tile([P, 2, P, PACK], BF16, name="w1_grouped", bufs=4, align_bytes=64)
                dst = grouped[:].rearrange("p t q j -> p q j t")
                src = w1_raw[b, a][:].rearrange("p j (q t) -> p q j t", t=PACK)[:, :, :, 2 * pair : 2 * pair + 2]
                if engine == "vector":
                    nc.vector.tensor_copy(dst, src)
                else:
                    nc.scalar.copy(dst, src)
                pairs.append(grouped)
            return pairs

        def quantise_w1(b, a, pairs):
            code = keep.tile([P, PACK, P], U32, name="w1_code%d%d" % (b, a), align_bytes=64)
            scale = keep.tile([P, PACK, P], U8, name="w1_scale%d%d" % (b, a), align_bytes=64)
            for pair, grouped in enumerate(pairs):
                slots = slice(2 * pair, 2 * pair + 2)
                nc.vector.quantize_mx(
                    out=code[:, slots, :].rearrange("p t q -> p (t q)").bitcast(FP8X4),
                    scales=scale[:, slots, :].rearrange("p t q -> p (t q)"),
                    in_=grouped[:].rearrange("p t q j -> p (t q j)"),
                )
            return code, scale

        def first_product(weights):
            banks = {}
            for half in range(HALVES):
                cols = slice(half * BANK, (half + 1) * BANK)
                for a, (code, scale) in enumerate(weights):
                    for t in range(PACK):
                        if a == 0:
                            banks[half, t] = psum.tile([P, BANK], F32, name="bank%d%d" % (half, t))
                        nc.tensor.matmul_mx(
                            out=banks[half, t][:],
                            lhsT=code[:, t, :].bitcast(FP8X4),
                            lhsT_scale=scale[:, t, :],
                            rhs=v_code[a][:, cols].bitcast(FP8X4),
                            rhs_scale=v_scale[a][:, cols],
                            start=(a == 0),
                            stop=(a == KP - 1),
                        )
            return banks

        def activate(b, banks):
            acts = []
            for half in range(HALVES):
                c0 = 0
                for width in H_PIECES[b][half]:
                    act = ring.tile([P, PACK, width], F32, name="act", bufs=3)
                    for t in range(PACK):
                        nc.scalar.activation(
                            act[:, t, :],
                            banks[half, t][:, c0 : c0 + width],
                            ACT.Gelu_apprx_tanh,
                            bias=shift_t[:, b, t : t + 1],
                        )
                    acts.append((half, c0, width, act))
                    c0 = c0 + width
            return acts

        h_code, h_scale = {}, {}

        def quantise_h(b, acts):
            factor = gain_t[:, b, :].rearrange("p (c t i) -> p c t i", c=1, i=1)
            for half in range(HALVES):
                h_code[b, half] = keep.tile([P, BANK], U32, name="h_code%d%d" % (b, half), align_bytes=64)
                h_scale[b, half] = keep.tile([P, BANK], U8, name="h_scale%d%d" % (b, half), align_bytes=64)
                if (b, half) == (0, 1):
                    h_bf = keep.tile([P, BANK, PACK], BF16, name="h_after", tag="handover", align_bytes=64)
                else:
                    h_bf = ring.tile([P, BANK, PACK], BF16, name="h_bf", bufs=2, align_bytes=64)
                for act_half, c0, width, act in acts:
                    if act_half == half:
                        for s0 in range(0, width, H_STEP):
                            nc.vector.tensor_tensor(
                                h_bf[:, c0 + s0 : c0 + s0 + H_STEP, :].rearrange("p (c i) t -> p c t i", i=2),
                                act[:, :, s0 : s0 + H_STEP].rearrange("p t (c i) -> p c t i", i=2),
                                factor.to_broadcast([P, H_STEP // 2, PACK, 2]),
                                ALU.mult,
                            )
                for s0 in range(0, BANK, H_STEP):
                    cols = slice(s0, s0 + H_STEP)
                    nc.vector.quantize_mx(
                        out=h_code[b, half][:, cols].bitcast(FP8X4),
                        scales=h_scale[b, half][:, cols],
                        in_=h_bf[:, cols, :].rearrange("p n t -> p (n t)"),
                    )

        banks0 = first_product([quantise_w1(0, a, round_w1(0, a)) for a in range(KP)])
        weights1 = [quantise_w1(1, 0, round_w1(1, 0))]
        rounded = [round_w1(1, a) for a in range(1, KP)]
        weights1.extend(quantise_w1(1, a, rounded[a - 1]) for a in range(1, KP))
        acts0 = activate(0, banks0)
        banks1 = first_product(weights1)
        quantise_h(0, acts0)
        quantise_h(1, activate(1, banks1))

        g2 = [keep.tile([P, S], F32, name="g2_%d" % t) for t in range(PACK)]
        for half in range(HALVES):
            for t in range(PACK):
                bank = psum.tile([P, BANK], F32, name="bank%d%d" % (half, t))
                for b in range(HP):
                    nc.tensor.matmul_mx(
                        out=bank[:],
                        lhsT=w4_code[:, b, t].rearrange("p q e -> p (q e)").bitcast(FP4X4),
                        lhsT_scale=w4_scale[:, b, t, :],
                        rhs=h_code[b, half][:].bitcast(FP8X4),
                        rhs_scale=h_scale[b, half][:],
                        start=(b == 0),
                        stop=(b == HP - 1),
                    )
                nc.scalar.activation(g2[t][:, half * BANK : (half + 1) * BANK], bank[:], ACT.Square)

        y_code = keep.tile([P, M], U32, name="y_code", align_bytes=64)
        y_scale = keep.tile([P, M], U8, name="y_scale", align_bytes=64)
        y_rows = out_0.rearrange("(p t) m -> p t m", t=PACK)
        code_rows = out_1[0].rearrange("p m t -> p (m t)").bitcast(I32)
        m0 = 0
        first = {}
        for piece, width in enumerate(M_PIECES):
            cols = slice(m0, m0 + width)
            lists = slice(m0 // 16, (m0 + width) // 16)
            m0 = m0 + width
            y = keep.tile([P, PACK, width], F32, name="y%d" % piece)
            for t in range(PACK):
                if piece == 0:
                    first[t] = keep.tile([P, M], F32, name="first%d" % t)
                    nc.vector.tensor_copy(first[t][:], g2[t][:].indirect(lead[:]))
                both = keep.tile([P, width], F32, name="both%d" % ((t + 2 * piece) % PACK))
                nc.vector.tensor_tensor(both[:], g2[t][:].indirect(trail[:, lists]), first[t][:, cols], ALU.add)
                nc.scalar.activation(y[:, t, :], both[:], ACT.Sqrt, bias=1.0)
            nc.sync.dma_start(y_rows[:, :, cols], y[:])
            y_bf = ring.tile([P, width, PACK], BF16, name="y_bf", bufs=2, align_bytes=64)
            dst = y_bf[:].rearrange("p (c i) t -> p c t i", i=2)
            src = y[:].rearrange("p t (c i) -> p c t i", i=2)
            if piece == len(M_PIECES) - 1:
                nc.vector.tensor_copy(dst, src)
            else:
                nc.scalar.copy(dst, src)
            nc.vector.quantize_mx(
                out=y_code[:, cols].bitcast(FP8X4),
                scales=y_scale[:, cols],
                in_=y_bf[:].rearrange("p m t -> p (m t)"),
            )
            nc.sync.dma_start(code_rows[:, cols], y_code[:, cols].bitcast(I32))
        for q in range(QUADS):
            queue = nc.scalar if q % 2 else nc.sync
            queue.dma_start(out_2[0, 4 * q : 4 * q + 4, :].bitcast(I32), y_scale[32 * q : 32 * q + 4, :].bitcast(I32))
